import numpy as np
import ml_dtypes


def mxq(x, axis, fmt="e4m3"):
    dtype, down = {"e4m3": (ml_dtypes.float8_e4m3fn, 7), "e5m2": (ml_dtypes.float8_e5m2, 14)}[fmt]
    v = np.moveaxis(np.asarray(x, np.float32).astype(ml_dtypes.bfloat16).astype(np.float64), axis, -1)
    blocks = v.reshape(v.shape[:-1] + (-1, 32))
    amax = np.abs(blocks).max(-1, keepdims=True)
    byte = np.maximum(np.where(amax > 0, np.frexp(amax)[1] - 1 + 127, 0) - down, 1)
    scale = np.exp2(byte - 127.0)
    codes = (blocks / scale).astype(np.float32).astype(dtype).astype(np.float64)
    return np.moveaxis((codes * scale).reshape(v.shape), -1, axis)


WIDE = False


def mx_kscale(k):
    if not WIDE:
        return np.ones(k)
    levels = np.array([10, -10, 5, -5, 0])
    if k % 512:
        return np.exp2(np.random.permutation(np.resize(levels, k // 32))).repeat(32)
    a = np.empty((k // 512, 16))
    for p in range(k // 512):
        a[p, :8] = np.random.permutation(np.resize(levels, 8))
        for g in range(8):
            far = levels[np.abs(levels - a[p, g]) >= 10]
            a[p, g + 8] = far[np.random.randint(len(far))]
    return np.exp2(a.ravel()).repeat(32)


BF16 = ml_dtypes.bfloat16


def bf(x):
    return np.asarray(x, np.float32).astype(BF16)


def f64(x):
    return np.asarray(x).astype(np.float64)


E2M1 = np.array([0.0, 0.5, 1.0, 1.5, 2.0, 3.0, 4.0, 6.0, -0.0, -0.5, -1.0, -1.5, -2.0, -3.0, -4.0, -6.0])


def pack_weight(w, fmt):
    k, n = w.shape
    w = f64(bf(w)).reshape(k // 32, 32, n)
    amax = np.abs(w).max(1)
    if fmt == "e4m3":
        byte = np.frexp(amax)[1] - 1 + 127 - 7
    else:
        mant, ex = np.frexp(amax / 6.0)
        byte = np.where(mant > 0.5, ex, ex - 1) + 127
    byte = np.clip(np.where(amax > 0, byte, 1), 1, 254)
    scaled = (w * np.exp2(127.0 - byte)[:, None, :]).reshape(k, n).astype(np.float32)
    by_word = np.ascontiguousarray(scaled.reshape(k // 512, 128, 4, n).transpose(0, 1, 3, 2))
    if fmt == "e4m3":
        words = by_word.astype(ml_dtypes.float8_e4m3fn).view(np.uint8)
    else:
        c = by_word.astype(ml_dtypes.float4_e2m1fn).view(np.uint8) & 0xF
        words = c[..., 0::2] | (c[..., 1::2] << 4)
    return np.ascontiguousarray(words), np.ascontiguousarray(byte.astype(np.uint8).reshape(k // 512, 16, n))


def unpack_weight(words, scales, fmt):
    g, p, n, _ = words.shape
    if fmt == "e4m3":
        vals = np.ascontiguousarray(words).view(ml_dtypes.float8_e4m3fn).astype(np.float64)
    else:
        nib = np.empty((g, p, n, 4), np.uint8)
        nib[..., 0::2] = words & 0xF
        nib[..., 1::2] = words >> 4
        vals = E2M1[nib]
    vals = vals * np.repeat(np.exp2(scales.astype(np.float64) - 127.0), 8, axis=1)[..., None]
    return vals.transpose(0, 1, 3, 2).reshape(g * 512, n)
def pack4(w):
    words, scales = pack_weight(w, "e2m1")
    return words.reshape(words.shape[0], 128, -1), scales


def unpack4(words, scales):
    return unpack_weight(words.reshape(words.shape[0], 128, -1, 2), scales, "e2m1")


def planes(Y):
    n, m = Y.shape
    b = f64(bf(Y)).reshape(n // 32, 32, m)
    amax = np.abs(b).max(1)
    byte = np.clip(np.where(amax > 0, np.frexp(amax)[1] - 1 + 127 - 7, 1), 1, 254)
    codes = (b * np.exp2(127.0 - byte)[:, None, :]).reshape(n, m).astype(np.float32).astype(ml_dtypes.float8_e4m3fn).view(np.uint8)
    words = codes.reshape(n // 512, 128, 4, m).transpose(0, 1, 3, 2)
    return np.ascontiguousarray(words), np.ascontiguousarray(byte.astype(np.uint8).reshape(n // 512, 16, m))


M, K, N = 768, 1536, 1024
LEVEL_A, LEVEL_B, LEVEL_D = 1.0, 0.8, 0.6

def setup_inputs():
    s = mx_kscale(K)[:, None]
    vol = np.exp(0.4 * np.random.randn(N))[None, :]
    x = np.random.randn(K, M)
    x = x / np.sqrt(np.mean(x ** 2, axis=0, keepdims=True))
    x_words, x_scales = pack_weight(f64(bf(x * s)), "e4m3")
    a = LEVEL_A * np.random.randn(K, N) * vol / np.sqrt(K)
    b = LEVEL_B * np.random.randn(K, N) * vol / np.sqrt(K)
    d = LEVEL_D * np.random.randn(K, N) * vol / np.sqrt(K)
    a_words, a_scales = pack_weight(f64(bf(a / s)), "e4m3")
    b_words, b_scales = pack4(f64(bf(b / s)))
    return {"x_words": x_words, "x_scales": x_scales, "a_words": a_words, "a_scales": a_scales,
            "b_words": b_words, "b_scales": b_scales, "d": bf(d / s)}

def reference(x_words, x_scales, a_words, a_scales, b_words, b_scales, d):
    x = unpack_weight(x_words, x_scales, "e4m3").T
    aw = unpack_weight(a_words, a_scales, "e4m3")
    bw = unpack4(b_words, b_scales)
    dw = mxq(f64(d), 0, "e4m3")
    impact = x @ aw
    frozen = x @ bw
    update = x @ dw
    y = np.square(impact) + np.square(frozen + update)
    Y = y.T
    words, scales = planes(Y)
    return y, words, scales

@@ -1,0 +1,363 @@
+from contextlib import ExitStack
+
+import concourse.mybir as mybir
+from concourse.masks import make_identity
+
+M, K, N = 768, 1536, 1024
+FLOPS = 3 * 2 * M * K * N
+
+F32 = mybir.dt.float32
+BF16 = mybir.dt.bfloat16
+I32 = mybir.dt.int32
+U32 = mybir.dt.uint32
+U8 = mybir.dt.uint8
+FP8X4 = mybir.dt.float8_e4m3fn_x4
+FP4X4 = mybir.dt.float4_e2m1fn_x4
+SQUARE = mybir.ActivationFunctionType.Square
+ADD = mybir.AluOpType.add
+
+P = 128
+PACK = 4
+GROUPS = K // (P * PACK)
+W = 512
+HALVES = N // W
+ROWS = M // P
+TILES = HALVES * ROWS
+LAST = TILES - 1
+CHUNK = 256
+SWEEP = 4
+VECTOR_SHARE = 320
+
+
+def tile_two_horizon_variance_contributions_k3_kernel(
+    tc, x_words, x_scales, a_words, a_scales, b_words, b_scales, d, out_0, out_1, out_2
+):
+    nc = tc.nc
+    with ExitStack() as ctx:
+        keep = ctx.enter_context(tc.tile_pool(name="keep", bufs=1))
+        work = ctx.enter_context(tc.tile_pool(name="work", bufs=3))
+        psum = ctx.enter_context(tc.psum_pool(name="psum", bufs=8))
+        ctx.enter_context(tc.manual_schedule())
+
+        def kept(name, shape, dtype):
+            return keep.tile(shape, dtype, name=name, align_bytes=256)
+
+        x_plane = kept("x_plane", [P, GROUPS, M], U8)
+        a_plane = kept("a_plane", [P, GROUPS, N], U8)
+        b_plane = kept("b_plane", [P, GROUPS, N], U8)
+        for plane in (x_plane, a_plane, b_plane):
+            nc.vector.memset(plane[:].bitcast(I32), 0)
+
+        def load_scale_rows(queue, plane, scales, quadrant):
+            queue.dma_start(
+                out=plane[32 * quadrant : 32 * quadrant + 4, :, :].bitcast(I32),
+                in_=scales[:, 4 * quadrant : 4 * quadrant + 4, :].rearrange("g r n -> r g n").bitcast(I32),
+            )
+
+        def load_words(name, words, g, first, count):
+            codes = kept(name, [P, count], U32)
+            row = words[g].rearrange("p n t -> p (n t)")
+            nc.sync.dma_start(out=codes[:].bitcast(I32), in_=row[:, PACK * first : PACK * (first + count)].bitcast(I32))
+            return codes
+
+        x_codes = {}
+        a_codes = {}
+        b_codes = {}
+        d_rows = {}
+
+        def load_x(g, first_row, rows):
+            codes = load_words("x_codes_%d_%d" % (g, first_row), x_words, g, P * first_row, P * rows)
+            for r in range(rows):
+                x_codes[g, first_row + r] = codes[:, P * r : P * (r + 1)]
+
+        def load_a(g, h):
+            a_codes[g, h] = load_words("a_codes_%d_%d" % (g, h), a_words, g, W * h, W)
+
+        def load_all_groups(name, words, first, count):
+            codes = kept(name, [P, GROUPS, count], U32)
+            rows = words.rearrange("g p n t -> p g (n t)")
+            nc.sync.dma_start(out=codes[:].bitcast(I32), in_=rows[:, :, PACK * first : PACK * (first + count)].bitcast(I32))
+            return codes
+
+        def load_b(h):
+            codes = kept("b_codes_%d" % h, [P, GROUPS, 2 * W], U8)
+            nc.sync.dma_start(
+                out=codes[:].bitcast(I32),
+                in_=b_words[:, :, 2 * W * h : 2 * W * (h + 1)].rearrange("g p n -> p g n").bitcast(I32),
+            )
+            b_codes[h] = codes
+
+        def load_d(g, h):
+            rows = kept("d_rows_%d_%d" % (g, h), [P, PACK, W], BF16)
+            nc.sync.dma_start(
+                out=rows[:],
+                in_=d[P * PACK * g : P * PACK * (g + 1), W * h : W * (h + 1)].rearrange("(p t) n -> p t n", t=PACK),
+            )
+            d_rows[g, h] = rows
+
+        for quadrant in range(4):
+            load_scale_rows(nc.scalar, x_plane, x_scales, quadrant)
+        load_x(0, 0, SWEEP)
+        load_a(0, 0)
+        for quadrant in range(4):
+            load_scale_rows(nc.sync if quadrant < 2 else nc.scalar, a_plane, a_scales, quadrant)
+        for quadrant in range(4):
+            load_scale_rows(nc.gpsimd, b_plane, b_scales, quadrant)
+        load_x(1, 0, SWEEP)
+        load_a(1, 0)
+        load_x(2, 0, SWEEP)
+        load_a(2, 0)
+        load_b(0)
+        load_d(0, 0)
+        load_d(1, 0)
+        load_d(2, 0)
+        x_rest = load_all_groups("x_rest", x_words, P * SWEEP, P * (ROWS - SWEEP))
+        for g in range(GROUPS):
+            for r in range(SWEEP, ROWS):
+                x_codes[g, r] = x_rest[:, g, P * (r - SWEEP) : P * (r - SWEEP + 1)]
+        load_d(0, 1)
+        load_d(1, 1)
+        a_rest = load_all_groups("a_rest", a_words, W, W)
+        for g in range(GROUPS):
+            a_codes[g, 1] = a_rest[:, g, :]
+        load_d(2, 1)
+        load_b(1)
+
+        identity = kept("identity", [P, P], F32)
+        make_identity(nc, identity[:])
+        table_warm = kept("table_warm", [P, 1], F32)
+        nc.scalar.activation(out=table_warm[:], in_=identity[:, 0:1], func=SQUARE)
+
+        d_codes = {(g, h): kept("d_codes_%d_%d" % (g, h), [P, W], U32) for g in range(GROUPS) for h in range(HALVES)}
+        d_plane = {(g, h): kept("d_plane_%d_%d" % (g, h), [P, W], U8) for g in range(GROUPS) for h in range(HALVES)}
+        d_grouped = {}
+
+        def interleave_d(copy, g, h, first, end):
+            copy(
+                out=d_grouped[g, h][:, first:end, :].rearrange("p (c i) t -> p c t i", i=4),
+                in_=d_rows[g, h][:, :, first:end].rearrange("p t (c i) -> p c t i", i=4),
+            )
+
+        def quantize_d(g, h, c):
+            cols = slice(CHUNK * c, CHUNK * (c + 1))
+            nc.vector.quantize_mx(
+                out=d_codes[g, h][:, cols].bitcast(FP8X4),
+                scales=d_plane[g, h][:, cols],
+                in_=d_grouped[g, h][:, cols, :].rearrange("p n t -> p (n t)"),
+            )
+
+        def mx_pass(bank, tile, g, rhs, rhs_scale, start, stop):
+            r = tile % ROWS
+            nc.tensor.matmul_mx(
+                out=bank,
+                lhsT=x_codes[g, r].bitcast(FP8X4),
+                lhsT_scale=x_plane[:, g, P * r : P * (r + 1)],
+                rhs=rhs,
+                rhs_scale=rhs_scale,
+                start=start,
+                stop=stop,
+            )
+
+        def impact_pass(bank, tile, g, first, count):
+            h = tile // ROWS
+            mx_pass(
+                bank[:, 0:count], tile, g,
+                a_codes[g, h][:, first : first + count].bitcast(FP8X4),
+                a_plane[:, g, W * h + first : W * h + first + count],
+                g == 0, g == GROUPS - 1,
+            )
+
+        def new_bank():
+            return psum.tile([P, W], F32, name="bank")
+
+        impact_sq = {}
+        horizon1_bank = {}
+        y_sorted = {}
+
+        def square_impact(tile, bank):
+            impact_sq[tile] = kept("impact_sq_%d" % tile, [P, W], F32)
+            nc.scalar.activation(out=impact_sq[tile][:], in_=bank[:], func=SQUARE)
+
+        def frozen_pass(tile, g):
+            h = tile // ROWS
+            mx_pass(
+                horizon1_bank[tile][:], tile, g,
+                b_codes[h][:, g, :].bitcast(FP4X4), b_plane[:, g, W * h : W * (h + 1)],
+                g == 0, False,
+            )
+
+        def update_pass(tile, g):
+            h = tile // ROWS
+            mx_pass(
+                horizon1_bank[tile][:], tile, g,
+                d_codes[g, h][:].bitcast(FP8X4), d_plane[g, h][:],
+                False, g == GROUPS - 1,
+            )
+
+        horizon1_sq = {}
+        y = {}
+
+        def square_horizon1(tile):
+            horizon1_sq[tile] = kept("horizon1_sq_%d" % tile, [P, W], F32)
+            nc.scalar.activation(out=horizon1_sq[tile][:], in_=horizon1_bank[tile][:], func=SQUARE)
+
+        def impact(tile):
+            bank = new_bank()
+            for g in range(GROUPS):
+                impact_pass(bank, tile, g, 0, W)
+            square_impact(tile, bank)
+
+        def frozen(tile):
+            horizon1_bank[tile] = new_bank()
+            for g in range(GROUPS):
+                frozen_pass(tile, g)
+
+        def update(tile):
+            for g in range(GROUPS):
+                update_pass(tile, g)
+            square_horizon1(tile)
+
+        def prepare_d(g, h):
+            d_grouped[g, h] = work.tile([P, W, PACK], BF16, name="d_grouped", align_bytes=256)
+            if h == 0:
+                interleave_d(nc.vector.tensor_copy, g, h, 0, VECTOR_SHARE)
+                interleave_d(nc.scalar.copy, g, h, VECTOR_SHARE, W)
+            else:
+                interleave_d(nc.vector.tensor_copy, g, h, 0, CHUNK)
+                interleave_d(nc.vector.tensor_copy, g, h, CHUNK, W)
+            for c in range(W // CHUNK):
+                quantize_d(g, h, c)
+
+        def finish(tiles):
+            for tile in tiles:
+                y[tile] = kept("y_%d" % tile, [P, W], F32)
+                nc.vector.tensor_tensor(out=y[tile][:], in0=impact_sq[tile][:], in1=horizon1_sq[tile][:], op=ADD)
+                store_y(tile, y[tile])
+            for tile in tiles:
+                y_sorted[tile] = kept("y_sorted_%d" % tile, [P, 2, P, 2], BF16)
+                nc.vector.tensor_copy(out=y_sorted[tile][:], in_=by_word(y[tile][:]))
+
+        def turn_and_quantize(batches):
+            turned = [turn(tiles) for tiles in batches]
+            for tiles, bank in zip(batches, turned):
+                planes(tiles, bank)
+
+        def store_y(tile, values):
+            h, r = divmod(tile, ROWS)
+            nc.sync.dma_start(out=out_0[P * r : P * (r + 1), W * h : W * (h + 1)], in_=values[:])
+
+        def by_word(ap):
+            return ap.rearrange("i (p u e) -> i u p e", u=2, e=2)
+
+        y_codes = [kept("y_codes_%d" % h, [P, M], U32) for h in range(HALVES)]
+        y_plane = [kept("y_plane_%d" % h, [P, M], U8) for h in range(HALVES)]
+
+        def turn(tiles):
+            bank = new_bank()
+            for n, tile in enumerate(tiles):
+                words = y_sorted[tile][:].rearrange("i u p e -> i u (p e)").bitcast(F32)
+                for u in range(2):
+                    nc.tensor.transpose(bank[:, P * (2 * n + u) : P * (2 * n + u + 1)], words[:, u, :], identity[:])
+            return bank
+
+        def planes(tiles, bank):
+            h, r = divmod(tiles[0], ROWS)
+            count = len(tiles)
+            grouped = work.tile([P, count * P * PACK], BF16, name="y_grouped", align_bytes=256)
+            nc.scalar.copy(
+                out=grouped[:].bitcast(F32).rearrange("p (n i u) -> p n i u", n=count, u=2),
+                in_=bank[:, 0 : 2 * P * count].rearrange("p (n u i) -> p n i u", n=count, u=2),
+            )
+            cols = slice(P * r, P * (r + count))
+            nc.vector.quantize_mx(out=y_codes[h][:, cols].bitcast(FP8X4), scales=y_plane[h][:, cols], in_=grouped[:])
+
+        def store_words(h, first_row, rows):
+            row = out_1[h].rearrange("p m t -> p (m t)")
+            nc.sync.dma_start(
+                out=row[:, PACK * P * first_row : PACK * P * (first_row + rows)].bitcast(I32),
+                in_=y_codes[h][:, P * first_row : P * (first_row + rows)].bitcast(I32),
+            )
+
+        def store_scales(h, queues):
+            for quadrant in range(4):
+                queues[quadrant % len(queues)].dma_start(
+                    out=out_2[h, 4 * quadrant : 4 * quadrant + 4, :].bitcast(I32),
+                    in_=y_plane[h][32 * quadrant : 32 * quadrant + 4, :].bitcast(I32),
+                )
+
+        sweep = range(SWEEP)
+        impact_banks = [new_bank() for tile in sweep]
+        for g in range(GROUPS):
+            for tile in sweep:
+                impact_pass(impact_banks[tile], tile, g, 0, W)
+        for tile in sweep:
+            horizon1_bank[tile] = new_bank()
+        for g in range(GROUPS):
+            for tile in sweep:
+                frozen_pass(tile, g)
+        prepare_d(0, 0)
+        square_impact(0, impact_banks[0])
+        for tile in sweep:
+            update_pass(tile, 0)
+        prepare_d(1, 0)
+        square_impact(1, impact_banks[1])
+        for tile in sweep:
+            update_pass(tile, 1)
+        prepare_d(2, 0)
+        square_impact(2, impact_banks[2])
+        square_impact(3, impact_banks[3])
+        impact(4)
+        for tile in sweep:
+            update_pass(tile, 2)
+            square_horizon1(tile)
+
+        prepare_d(0, 1)
+        frozen(4); update(4)
+        finish([0, 1])
+        prepare_d(1, 1)
+        impact(5); frozen(5); update(5)
+        finish([2, 3])
+        prepare_d(2, 1)
+        impact(6); frozen(6)
+        finish([4, 5])
+        impact(7); frozen(7)
+        update(6)
+        update(7)
+        turn_and_quantize([(0, 1), (2, 3), (4, 5)])
+        store_words(0, 0, ROWS)
+        store_scales(0, [nc.sync])
+        finish([6, 7])
+        impact(8); frozen(8); update(8)
+        finish([8])
+        impact(9); frozen(9); update(9)
+        finish([9])
+        impact(10); frozen(10); update(10)
+        finish([10])
+
+        frozen(LAST)
+        update(LAST)
+        early, late = turn((6, 7)), turn((8, 9))
+        planes((6, 7), early)
+        store_words(1, 0, 2)
+        y[LAST] = kept("y_last", [P, W], F32)
+        y_sorted[LAST] = kept("y_sorted_%d" % LAST, [P, 2, P, 2], BF16)
+        last_sq = kept("last_sq", [P, W], F32)
+        part = W // 2
+        for c in range(2):
+            bank = new_bank()
+            for g in range(GROUPS):
+                impact_pass(bank, LAST, g, part * c, part)
+            cols = slice(part * c, part * (c + 1))
+            nc.scalar.activation(out=last_sq[:, cols], in_=bank[:, 0:part], func=SQUARE)
+            nc.vector.tensor_tensor(
+                out=y_sorted[LAST][:, :, P // 2 * c : P // 2 * (c + 1), :],
+                in0=by_word(last_sq[:, cols]), in1=by_word(horizon1_sq[LAST][:, cols]), op=ADD,
+            )
+        nc.vector.tensor_tensor(out=y[LAST][:], in0=last_sq[:], in1=horizon1_sq[LAST][:], op=ADD)
+        store_y(LAST, y[LAST])
+        planes((8, 9), late)
+        store_words(1, 2, 2)
+        turn_and_quantize([(10,)])
+        turn_and_quantize([(LAST,)])
+        store_words(1, 4, 2)
+        store_scales(1, [nc.scalar, nc.sync])

@@ -17,6 +17,8 @@ SQUARE = mybir.ActivationFunctionType.Square
 ADD = mybir.AluOpType.add
 
 P = 128
+QUAD = 32
+QUADS = P // QUAD
 PACK = 4
 GROUPS = K // (P * PACK)
 W = 512
@@ -24,9 +26,11 @@ HALVES = N // W
 ROWS = M // P
 TILES = HALVES * ROWS
 LAST = TILES - 1
+MIXED = 4
 CHUNK = 256
-SWEEP = 4
 VECTOR_SHARE = 320
+A_ROW = 4
+PORT_ORDER = (0, 2, 1, 3)
 
 
 def tile_two_horizon_variance_contributions_k3_kernel(
@@ -48,135 +52,124 @@ def tile_two_horizon_variance_contributions_k3_kernel(
         for plane in (x_plane, a_plane, b_plane):
             nc.vector.memset(plane[:].bitcast(I32), 0)
 
-        def load_scale_rows(queue, plane, scales, quadrant):
-            queue.dma_start(
-                out=plane[32 * quadrant : 32 * quadrant + 4, :, :].bitcast(I32),
-                in_=scales[:, 4 * quadrant : 4 * quadrant + 4, :].rearrange("g r n -> r g n").bitcast(I32),
-            )
+        def load_scale_rows(queue, plane, row, scales, quads):
+            for q in quads:
+                queue.dma_start(
+                    out=plane[QUAD * q + row : QUAD * q + row + 4, :, :].bitcast(I32),
+                    in_=scales[:, 4 * q : 4 * q + 4, :].rearrange("g r n -> r g n").bitcast(I32),
+                )
 
-        def load_words(name, words, g, first, count):
-            codes = kept(name, [P, count], U32)
-            row = words[g].rearrange("p n t -> p (n t)")
-            nc.sync.dma_start(out=codes[:].bitcast(I32), in_=row[:, PACK * first : PACK * (first + count)].bitcast(I32))
+        def load_words(name, words, groups, first, count):
+            codes = kept(name, [P, len(groups), count], U32)
+            rows = words[groups.start : groups.stop].rearrange("g p n t -> p g (n t)")
+            nc.sync.dma_start(out=codes[:].bitcast(I32), in_=rows[:, :, PACK * first : PACK * (first + count)].bitcast(I32))
             return codes
 
-        x_codes = {}
         a_codes = {}
         b_codes = {}
         d_rows = {}
 
-        def load_x(g, first_row, rows):
-            codes = load_words("x_codes_%d_%d" % (g, first_row), x_words, g, P * first_row, P * rows)
-            for r in range(rows):
-                x_codes[g, first_row + r] = codes[:, P * r : P * (r + 1)]
-
-        def load_a(g, h):
-            a_codes[g, h] = load_words("a_codes_%d_%d" % (g, h), a_words, g, W * h, W)
-
-        def load_all_groups(name, words, first, count):
-            codes = kept(name, [P, GROUPS, count], U32)
-            rows = words.rearrange("g p n t -> p g (n t)")
-            nc.sync.dma_start(out=codes[:].bitcast(I32), in_=rows[:, :, PACK * first : PACK * (first + count)].bitcast(I32))
-            return codes
+        def load_a(groups, h):
+            codes = load_words("a_codes_%d_%d" % (groups.start, h), a_words, groups, W * h, W)
+            for i, g in enumerate(groups):
+                a_codes[g, h] = codes[:, i, :]
 
         def load_b(h):
-            codes = kept("b_codes_%d" % h, [P, GROUPS, 2 * W], U8)
+            b_codes[h] = kept("b_codes_%d" % h, [P, GROUPS, 2 * W], U8)
             nc.sync.dma_start(
-                out=codes[:].bitcast(I32),
+                out=b_codes[h][:].bitcast(I32),
                 in_=b_words[:, :, 2 * W * h : 2 * W * (h + 1)].rearrange("g p n -> p g n").bitcast(I32),
             )
-            b_codes[h] = codes
 
         def load_d(g, h):
-            rows = kept("d_rows_%d_%d" % (g, h), [P, PACK, W], BF16)
+            d_rows[g, h] = kept("d_rows_%d_%d" % (g, h), [P, PACK, W], BF16)
             nc.sync.dma_start(
-                out=rows[:],
+                out=d_rows[g, h][:],
                 in_=d[P * PACK * g : P * PACK * (g + 1), W * h : W * (h + 1)].rearrange("(p t) n -> p t n", t=PACK),
             )
-            d_rows[g, h] = rows
 
-        for quadrant in range(4):
-            load_scale_rows(nc.scalar, x_plane, x_scales, quadrant)
-        load_x(0, 0, SWEEP)
-        load_a(0, 0)
-        for quadrant in range(4):
-            load_scale_rows(nc.sync if quadrant < 2 else nc.scalar, a_plane, a_scales, quadrant)
-        for quadrant in range(4):
-            load_scale_rows(nc.gpsimd, b_plane, b_scales, quadrant)
-        load_x(1, 0, SWEEP)
-        load_a(1, 0)
-        load_x(2, 0, SWEEP)
-        load_a(2, 0)
+        load_scale_rows(nc.scalar, x_plane, 0, x_scales, PORT_ORDER)
+        x_early = load_words("x_early", x_words, range(0, 2), 0, MIXED * P)
+        load_a(range(0, 2), 0)
+        load_scale_rows(nc.sync, a_plane, A_ROW, a_scales, PORT_ORDER[:2])
+        load_scale_rows(nc.scalar, a_plane, A_ROW, a_scales, PORT_ORDER[2:])
+        x_late = load_words("x_late", x_words, range(2, 3), 0, MIXED * P)
+        load_a(range(2, 3), 0)
         load_b(0)
         load_d(0, 0)
-        load_d(1, 0)
-        load_d(2, 0)
-        x_rest = load_all_groups("x_rest", x_words, P * SWEEP, P * (ROWS - SWEEP))
-        for g in range(GROUPS):
-            for r in range(SWEEP, ROWS):
-                x_codes[g, r] = x_rest[:, g, P * (r - SWEEP) : P * (r - SWEEP + 1)]
-        load_d(0, 1)
-        load_d(1, 1)
-        a_rest = load_all_groups("a_rest", a_words, W, W)
-        for g in range(GROUPS):
-            a_codes[g, 1] = a_rest[:, g, :]
-        load_d(2, 1)
-        load_b(1)
-
         identity = kept("identity", [P, P], F32)
         make_identity(nc, identity[:])
         table_warm = kept("table_warm", [P, 1], F32)
         nc.scalar.activation(out=table_warm[:], in_=identity[:, 0:1], func=SQUARE)
+        load_scale_rows(nc.sync, b_plane, 0, b_scales, PORT_ORDER)
+        load_d(1, 0)
+        load_d(2, 0)
+        x_rest = load_words("x_rest", x_words, range(GROUPS), MIXED * P, (ROWS - MIXED) * P)
+        load_d(0, 1)
+        load_d(1, 1)
+        load_a(range(GROUPS), 1)
+        load_b(1)
+        load_d(2, 1)
+
+        mixed_codes = [kept("mixed_codes_%d" % g, [P, MIXED * P], U32) for g in range(GROUPS)]
+        mixed_plane = [kept("mixed_plane_%d" % g, [P, MIXED * P], U8) for g in range(GROUPS)]
+        for g, loaded in enumerate((x_early[:, 0, :], x_early[:, 1, :], x_late[:, 0, :])):
+            nc.vector.tensor_copy(
+                out=mixed_plane[g][:].rearrange("p (r i) -> p r i", r=MIXED),
+                in_=x_plane[:, g, 0 : MIXED * P].rearrange("p (i r) -> p r i", r=MIXED),
+            )
+            nc.vector.tensor_copy(
+                out=mixed_codes[g][:].bitcast(I32).rearrange("p (r i) -> p r i", r=MIXED),
+                in_=loaded.bitcast(I32).rearrange("p (i r) -> p r i", r=MIXED),
+            )
 
         d_codes = {(g, h): kept("d_codes_%d_%d" % (g, h), [P, W], U32) for g in range(GROUPS) for h in range(HALVES)}
         d_plane = {(g, h): kept("d_plane_%d_%d" % (g, h), [P, W], U8) for g in range(GROUPS) for h in range(HALVES)}
-        d_grouped = {}
 
-        def interleave_d(copy, g, h, first, end):
-            copy(
-                out=d_grouped[g, h][:, first:end, :].rearrange("p (c i) t -> p c t i", i=4),
-                in_=d_rows[g, h][:, :, first:end].rearrange("p t (c i) -> p c t i", i=4),
-            )
-
-        def quantize_d(g, h, c):
-            cols = slice(CHUNK * c, CHUNK * (c + 1))
-            nc.vector.quantize_mx(
-                out=d_codes[g, h][:, cols].bitcast(FP8X4),
-                scales=d_plane[g, h][:, cols],
-                in_=d_grouped[g, h][:, cols, :].rearrange("p n t -> p (n t)"),
-            )
+        def prepare_d(g, h):
+            grouped = work.tile([P, W, PACK], BF16, name="d_grouped", align_bytes=256)
+            split = VECTOR_SHARE if h == 0 else CHUNK
+            second = nc.scalar.copy if h == 0 else nc.vector.tensor_copy
+            for copy, cols in ((nc.vector.tensor_copy, slice(0, split)), (second, slice(split, W))):
+                copy(
+                    out=grouped[:, cols, :].rearrange("p (c i) t -> p c t i", i=4),
+                    in_=d_rows[g, h][:, :, cols].rearrange("p t (c i) -> p c t i", i=4),
+                )
+            for c in range(W // CHUNK):
+                cols = slice(CHUNK * c, CHUNK * (c + 1))
+                nc.vector.quantize_mx(
+                    out=d_codes[g, h][:, cols].bitcast(FP8X4),
+                    scales=d_plane[g, h][:, cols],
+                    in_=grouped[:, cols, :].rearrange("p n t -> p (n t)"),
+                )
 
         def mx_pass(bank, tile, g, rhs, rhs_scale, start, stop):
             r = tile % ROWS
+            cols = slice(P * r, P * (r + 1))
+            if r < MIXED:
+                codes, plane = mixed_codes[g][:, cols], mixed_plane[g][:, cols]
+            else:
+                codes, plane = x_rest[:, g, P * (r - MIXED) : P * (r - MIXED + 1)], x_plane[:, g, cols]
             nc.tensor.matmul_mx(
-                out=bank,
-                lhsT=x_codes[g, r].bitcast(FP8X4),
-                lhsT_scale=x_plane[:, g, P * r : P * (r + 1)],
-                rhs=rhs,
-                rhs_scale=rhs_scale,
-                start=start,
-                stop=stop,
+                out=bank, lhsT=codes.bitcast(FP8X4), lhsT_scale=plane, rhs=rhs, rhs_scale=rhs_scale, start=start, stop=stop
             )
+
+        def new_bank():
+            return psum.tile([P, W], F32, name="bank")
+
+        horizon1_bank = {}
+        impact_sq = {}
+        horizon1_sq = {}
+        y_sorted = {}
 
         def impact_pass(bank, tile, g, first, count):
             h = tile // ROWS
             mx_pass(
                 bank[:, 0:count], tile, g,
                 a_codes[g, h][:, first : first + count].bitcast(FP8X4),
-                a_plane[:, g, W * h + first : W * h + first + count],
+                a_plane[A_ROW:, g, W * h + first : W * h + first + count],
                 g == 0, g == GROUPS - 1,
             )
-
-        def new_bank():
-            return psum.tile([P, W], F32, name="bank")
-
-        impact_sq = {}
-        horizon1_bank = {}
-        y_sorted = {}
-
-        def square_impact(tile, bank):
-            impact_sq[tile] = kept("impact_sq_%d" % tile, [P, W], F32)
-            nc.scalar.activation(out=impact_sq[tile][:], in_=bank[:], func=SQUARE)
 
         def frozen_pass(tile, g):
             h = tile // ROWS
@@ -194,8 +187,9 @@ def tile_two_horizon_variance_contributions_k3_kernel(
                 False, g == GROUPS - 1,
             )
 
-        horizon1_sq = {}
-        y = {}
+        def square_impact(tile, bank):
+            impact_sq[tile] = kept("impact_sq_%d" % tile, [P, W], F32)
+            nc.scalar.activation(out=impact_sq[tile][:], in_=bank[:], func=SQUARE)
 
         def square_horizon1(tile):
             horizon1_sq[tile] = kept("horizon1_sq_%d" % tile, [P, W], F32)
@@ -217,75 +211,93 @@ def tile_two_horizon_variance_contributions_k3_kernel(
                 update_pass(tile, g)
             square_horizon1(tile)
 
-        def prepare_d(g, h):
-            d_grouped[g, h] = work.tile([P, W, PACK], BF16, name="d_grouped", align_bytes=256)
-            if h == 0:
-                interleave_d(nc.vector.tensor_copy, g, h, 0, VECTOR_SHARE)
-                interleave_d(nc.scalar.copy, g, h, VECTOR_SHARE, W)
-            else:
-                interleave_d(nc.vector.tensor_copy, g, h, 0, CHUNK)
-                interleave_d(nc.vector.tensor_copy, g, h, CHUNK, W)
-            for c in range(W // CHUNK):
-                quantize_d(g, h, c)
-
-        def finish(tiles):
-            for tile in tiles:
-                y[tile] = kept("y_%d" % tile, [P, W], F32)
-                nc.vector.tensor_tensor(out=y[tile][:], in0=impact_sq[tile][:], in1=horizon1_sq[tile][:], op=ADD)
-                store_y(tile, y[tile])
-            for tile in tiles:
-                y_sorted[tile] = kept("y_sorted_%d" % tile, [P, 2, P, 2], BF16)
-                nc.vector.tensor_copy(out=y_sorted[tile][:], in_=by_word(y[tile][:]))
-
-        def turn_and_quantize(batches):
-            turned = [turn(tiles) for tiles in batches]
-            for tiles, bank in zip(batches, turned):
-                planes(tiles, bank)
-
-        def store_y(tile, values):
-            h, r = divmod(tile, ROWS)
-            nc.sync.dma_start(out=out_0[P * r : P * (r + 1), W * h : W * (h + 1)], in_=values[:])
-
         def by_word(ap):
             return ap.rearrange("i (p u e) -> i u p e", u=2, e=2)
 
-        y_codes = [kept("y_codes_%d" % h, [P, M], U32) for h in range(HALVES)]
-        y_plane = [kept("y_plane_%d" % h, [P, M], U8) for h in range(HALVES)]
+        y = {}
 
-        def turn(tiles):
+        def add_squares(tile):
+            h, r = divmod(tile, ROWS)
+            y[tile] = kept("y_%d" % tile, [P, W], F32)
+            nc.vector.tensor_tensor(out=y[tile][:], in0=impact_sq[tile][:], in1=horizon1_sq[tile][:], op=ADD)
+            rows = out_0[r : MIXED * P : MIXED, :] if r < MIXED else out_0[P * r : P * (r + 1), :]
+            nc.sync.dma_start(out=rows[:, W * h : W * (h + 1)], in_=y[tile][:])
+
+        def round_y(tile):
+            y_sorted[tile] = kept("y_sorted_%d" % tile, [P, 2, P, 2], BF16)
+            nc.vector.tensor_copy(out=y_sorted[tile][:], in_=by_word(y[tile][:]))
+
+        def finish(tiles):
+            for tile in tiles:
+                add_squares(tile)
+            for tile in tiles:
+                round_y(tile)
+
+        def sorted_words(tile):
+            return y_sorted[tile][:].rearrange("i u p e -> i (u p e)").bitcast(F32)
+
+        mixed_grouped = [kept("mixed_grouped_%d" % h, [P, P, MIXED * PACK], BF16) for h in range(HALVES)]
+        turned = {}
+
+        def turn_blocks(tile):
+            if tile % 2 == 0:
+                turned[tile // 2] = kept("turned_%d" % tile, [P, 2, 2 * P], F32)
+            nc.vector.transpose(out=turned[tile // 2][:, tile % 2, :], in_=sorted_words(tile))
+
+        def pair_words(tile):
+            h, r = divmod(tile, ROWS)
+            nc.scalar.copy(
+                out=mixed_grouped[h][:].bitcast(F32)[:, :, 2 * r : 2 * r + 4],
+                in_=turned[tile // 2][:].rearrange("p r (u n) -> p n (r u)", u=2),
+            )
+
+        mixed_y_codes = kept("mixed_y_codes", [P, HALVES * QUADS, P], U32)
+        mixed_y_plane = kept("mixed_y_plane", [P, HALVES * QUADS, P], U8)
+
+        def quantize_mixed(h):
+            blocks = slice(QUADS * h, QUADS * (h + 1))
+            nc.vector.quantize_mx(
+                out=mixed_y_codes[:, blocks, :].rearrange("p b i -> p (b i)").bitcast(FP8X4),
+                scales=mixed_y_plane[:, blocks, :].rearrange("p b i -> p (b i)"),
+                in_=mixed_grouped[h][:].rearrange("p n w -> p (n w)"),
+            )
+
+        def store_mixed_planes():
+            words = out_1.rearrange("h (b c) m t -> c (h b) (m t)", b=QUADS)
+            scales = out_2.rearrange("h (b s) m -> s (h b) m", b=QUADS)
+            for q in PORT_ORDER:
+                nc.sync.dma_start(
+                    out=scales[:, :, P * q : P * (q + 1)].bitcast(I32),
+                    in_=mixed_y_plane[QUAD * q : QUAD * q + 4, :, :].bitcast(I32),
+                )
+            for q in PORT_ORDER:
+                nc.sync.dma_start(
+                    out=words[:, :, PACK * P * q : PACK * P * (q + 1)].bitcast(I32),
+                    in_=mixed_y_codes[QUAD * q : QUAD * (q + 1), :, :].bitcast(I32),
+                )
+
+        plain = (ROWS - MIXED) * P
+        plain_codes = kept("plain_y_codes", [P, HALVES, plain], U32)
+        plain_plane = kept("plain_y_plane", [P, HALVES, plain], U8)
+
+        def turn_whole(tiles):
             bank = new_bank()
             for n, tile in enumerate(tiles):
-                words = y_sorted[tile][:].rearrange("i u p e -> i u (p e)").bitcast(F32)
                 for u in range(2):
-                    nc.tensor.transpose(bank[:, P * (2 * n + u) : P * (2 * n + u + 1)], words[:, u, :], identity[:])
-            return bank
-
-        def planes(tiles, bank):
+                    nc.tensor.transpose(
+                        bank[:, P * (2 * n + u) : P * (2 * n + u + 1)], sorted_words(tile)[:, P * u : P * (u + 1)], identity[:]
+                    )
             h, r = divmod(tiles[0], ROWS)
             count = len(tiles)
-            grouped = work.tile([P, count * P * PACK], BF16, name="y_grouped", align_bytes=256)
+            grouped = work.tile([P, count * P * PACK], BF16, name="plain_grouped", align_bytes=256)
             nc.scalar.copy(
                 out=grouped[:].bitcast(F32).rearrange("p (n i u) -> p n i u", n=count, u=2),
                 in_=bank[:, 0 : 2 * P * count].rearrange("p (n u i) -> p n i u", n=count, u=2),
             )
-            cols = slice(P * r, P * (r + count))
-            nc.vector.quantize_mx(out=y_codes[h][:, cols].bitcast(FP8X4), scales=y_plane[h][:, cols], in_=grouped[:])
+            cols = slice(P * (r - MIXED), P * (r - MIXED + count))
+            nc.vector.quantize_mx(out=plain_codes[:, h, cols].bitcast(FP8X4), scales=plain_plane[:, h, cols], in_=grouped[:])
 
-        def store_words(h, first_row, rows):
-            row = out_1[h].rearrange("p m t -> p (m t)")
-            nc.sync.dma_start(
-                out=row[:, PACK * P * first_row : PACK * P * (first_row + rows)].bitcast(I32),
-                in_=y_codes[h][:, P * first_row : P * (first_row + rows)].bitcast(I32),
-            )
-
-        def store_scales(h, queues):
-            for quadrant in range(4):
-                queues[quadrant % len(queues)].dma_start(
-                    out=out_2[h, 4 * quadrant : 4 * quadrant + 4, :].bitcast(I32),
-                    in_=y_plane[h][32 * quadrant : 32 * quadrant + 4, :].bitcast(I32),
-                )
-
-        sweep = range(SWEEP)
+        sweep = range(MIXED)
         impact_banks = [new_bank() for tile in sweep]
         for g in range(GROUPS):
             for tile in sweep:
@@ -312,52 +324,82 @@ def tile_two_horizon_variance_contributions_k3_kernel(
             square_horizon1(tile)
 
         prepare_d(0, 1)
-        frozen(4); update(4)
-        finish([0, 1])
         prepare_d(1, 1)
-        impact(5); frozen(5); update(5)
-        finish([2, 3])
+        frozen(4)
+        update(4)
+        impact(6)
+        frozen(6)
+        add_squares(0)
+        add_squares(1)
+        add_squares(2)
         prepare_d(2, 1)
-        impact(6); frozen(6)
-        finish([4, 5])
-        impact(7); frozen(7)
+        impact(7)
+        frozen(7)
+        add_squares(3)
+        add_squares(4)
         update(6)
         update(7)
-        turn_and_quantize([(0, 1), (2, 3), (4, 5)])
-        store_words(0, 0, ROWS)
-        store_scales(0, [nc.sync])
+        impact(8)
+        for tile in sweep:
+            round_y(tile)
+        for tile in sweep:
+            turn_blocks(tile)
+        pair_words(0)
+        pair_words(2)
+        frozen(8)
+        update(8)
+        impact(9)
         finish([6, 7])
-        impact(8); frozen(8); update(8)
-        finish([8])
-        impact(9); frozen(9); update(9)
-        finish([9])
-        impact(10); frozen(10); update(10)
+        quantize_mixed(0)
+        add_squares(8)
+        turn_blocks(6)
+        turn_blocks(7)
+        round_y(8)
+        frozen(9)
+        update(9)
+        pair_words(6)
+        impact(5)
+        add_squares(9)
+        turn_blocks(8)
+        round_y(9)
+        round_y(4)
+        turn_blocks(9)
+        pair_words(8)
+        frozen(5)
+        update(5)
+        quantize_mixed(1)
+        store_mixed_planes()
+        impact(10)
+        finish([5])
+        frozen(10)
+        update(10)
         finish([10])
 
         frozen(LAST)
         update(LAST)
-        early, late = turn((6, 7)), turn((8, 9))
-        planes((6, 7), early)
-        store_words(1, 0, 2)
-        y[LAST] = kept("y_last", [P, W], F32)
         y_sorted[LAST] = kept("y_sorted_%d" % LAST, [P, 2, P, 2], BF16)
-        last_sq = kept("last_sq", [P, W], F32)
+        impact_sq[LAST] = kept("impact_sq_last", [P, W], F32)
         part = W // 2
         for c in range(2):
             bank = new_bank()
             for g in range(GROUPS):
                 impact_pass(bank, LAST, g, part * c, part)
             cols = slice(part * c, part * (c + 1))
-            nc.scalar.activation(out=last_sq[:, cols], in_=bank[:, 0:part], func=SQUARE)
+            nc.scalar.activation(out=impact_sq[LAST][:, cols], in_=bank[:, 0:part], func=SQUARE)
             nc.vector.tensor_tensor(
                 out=y_sorted[LAST][:, :, P // 2 * c : P // 2 * (c + 1), :],
-                in0=by_word(last_sq[:, cols]), in1=by_word(horizon1_sq[LAST][:, cols]), op=ADD,
+                in0=by_word(impact_sq[LAST][:, cols]), in1=by_word(horizon1_sq[LAST][:, cols]), op=ADD,
             )
-        nc.vector.tensor_tensor(out=y[LAST][:], in0=last_sq[:], in1=horizon1_sq[LAST][:], op=ADD)
-        store_y(LAST, y[LAST])
-        planes((8, 9), late)
-        store_words(1, 2, 2)
-        turn_and_quantize([(10,)])
-        turn_and_quantize([(LAST,)])
-        store_words(1, 4, 2)
-        store_scales(1, [nc.scalar, nc.sync])
+        add_squares(LAST)
+        turn_whole((4, 5))
+        turn_whole((10,))
+        turn_whole((LAST,))
+        nc.sync.dma_start(
+            out=out_1.rearrange("h p m t -> p h (m t)")[:, :, PACK * MIXED * P :].bitcast(I32),
+            in_=plain_codes[:].bitcast(I32),
+        )
+        for q in PORT_ORDER:
+            nc.scalar.dma_start(
+                out=out_2[:, 4 * q : 4 * q + 4, MIXED * P :].rearrange("h s m -> s h m").bitcast(I32),
+                in_=plain_plane[QUAD * q : QUAD * q + 4, :, :].bitcast(I32),
+            )

@@ -47,9 +47,9 @@ def tile_two_horizon_variance_contributions_k3_kernel(
             return keep.tile(shape, dtype, name=name, align_bytes=256)
 
         x_plane = kept("x_plane", [P, GROUPS, M], U8)
-        a_plane = kept("a_plane", [P, GROUPS, N], U8)
-        b_plane = kept("b_plane", [P, GROUPS, N], U8)
-        for plane in (x_plane, a_plane, b_plane):
+        a_plane = [kept("a_plane_%d" % h, [P, GROUPS, W], U8) for h in range(HALVES)]
+        b_plane = [kept("b_plane_%d" % h, [P, GROUPS, W], U8) for h in range(HALVES)]
+        for plane in (x_plane, a_plane[0], b_plane[0], a_plane[1], b_plane[1]):
             nc.vector.memset(plane[:].bitcast(I32), 0)
 
         def load_scale_rows(queue, plane, row, scales, quads):
@@ -88,32 +88,36 @@ def tile_two_horizon_variance_contributions_k3_kernel(
                 in_=d[P * PACK * g : P * PACK * (g + 1), W * h : W * (h + 1)].rearrange("(p t) n -> p t n", t=PACK),
             )
 
-        load_scale_rows(nc.scalar, x_plane, 0, x_scales, PORT_ORDER)
-        x_early = load_words("x_early", x_words, range(0, 2), 0, MIXED * P)
-        load_a(range(0, 2), 0)
-        load_scale_rows(nc.sync, a_plane, A_ROW, a_scales, PORT_ORDER[:2])
-        load_scale_rows(nc.scalar, a_plane, A_ROW, a_scales, PORT_ORDER[2:])
-        x_late = load_words("x_late", x_words, range(2, 3), 0, MIXED * P)
+        load_scale_rows(nc.sync, x_plane, 0, x_scales, (0,))
+        load_scale_rows(nc.scalar, x_plane, 0, x_scales, (2,))
+        load_scale_rows(nc.sync, x_plane, 0, x_scales, (1,))
+        load_scale_rows(nc.scalar, x_plane, 0, x_scales, (3,))
+        x_early = load_words("x_early", x_words, range(0, 1), 0, MIXED * P)
+        load_a(range(0, 1), 0)
+        load_scale_rows(nc.sync, a_plane[0], A_ROW, a_scales[:, :, 0:W], PORT_ORDER)
+        x_late = load_words("x_late", x_words, range(1, 3), 0, MIXED * P)
+        load_a(range(1, 2), 0)
         load_a(range(2, 3), 0)
         load_b(0)
-        load_d(0, 0)
+        load_scale_rows(nc.sync, b_plane[0], 0, b_scales[:, :, 0:W], PORT_ORDER)
+        for g in range(GROUPS):
+            load_d(g, 0)
+        x_rest = load_words("x_rest", x_words, range(GROUPS), MIXED * P, (ROWS - MIXED) * P)
+        load_d(0, 1)
+        load_d(1, 1)
+        load_scale_rows(nc.sync, a_plane[1], A_ROW, a_scales[:, :, W:], PORT_ORDER)
+        load_a(range(GROUPS), 1)
+        load_scale_rows(nc.sync, b_plane[1], 0, b_scales[:, :, W:], PORT_ORDER)
+        load_b(1)
+        load_d(2, 1)
         identity = kept("identity", [P, P], F32)
         make_identity(nc, identity[:])
         table_warm = kept("table_warm", [P, 1], F32)
         nc.scalar.activation(out=table_warm[:], in_=identity[:, 0:1], func=SQUARE)
-        load_scale_rows(nc.sync, b_plane, 0, b_scales, PORT_ORDER)
-        load_d(1, 0)
-        load_d(2, 0)
-        x_rest = load_words("x_rest", x_words, range(GROUPS), MIXED * P, (ROWS - MIXED) * P)
-        load_d(0, 1)
-        load_d(1, 1)
-        load_a(range(GROUPS), 1)
-        load_b(1)
-        load_d(2, 1)
 
         mixed_codes = [kept("mixed_codes_%d" % g, [P, MIXED * P], U32) for g in range(GROUPS)]
         mixed_plane = [kept("mixed_plane_%d" % g, [P, MIXED * P], U8) for g in range(GROUPS)]
-        for g, loaded in enumerate((x_early[:, 0, :], x_early[:, 1, :], x_late[:, 0, :])):
+        for g, loaded in enumerate((x_early[:, 0, :], x_late[:, 0, :], x_late[:, 1, :])):
             nc.vector.tensor_copy(
                 out=mixed_plane[g][:].rearrange("p (r i) -> p r i", r=MIXED),
                 in_=x_plane[:, g, 0 : MIXED * P].rearrange("p (i r) -> p r i", r=MIXED),
@@ -126,22 +130,22 @@ def tile_two_horizon_variance_contributions_k3_kernel(
         d_codes = {(g, h): kept("d_codes_%d_%d" % (g, h), [P, W], U32) for g in range(GROUPS) for h in range(HALVES)}
         d_plane = {(g, h): kept("d_plane_%d_%d" % (g, h), [P, W], U8) for g in range(GROUPS) for h in range(HALVES)}
 
-        def prepare_d(g, h):
-            grouped = work.tile([P, W, PACK], BF16, name="d_grouped", align_bytes=256)
-            split = VECTOR_SHARE if h == 0 else CHUNK
-            second = nc.scalar.copy if h == 0 else nc.vector.tensor_copy
-            for copy, cols in ((nc.vector.tensor_copy, slice(0, split)), (second, slice(split, W))):
+        d_grouped = {}
+
+        def interleave_d(g, h):
+            d_grouped[g, h] = work.tile([P, W, PACK], BF16, name="d_grouped", align_bytes=256)
+            for copy, cols in ((nc.vector.tensor_copy, slice(0, VECTOR_SHARE)), (nc.scalar.copy, slice(VECTOR_SHARE, W))):
                 copy(
-                    out=grouped[:, cols, :].rearrange("p (c i) t -> p c t i", i=4),
+                    out=d_grouped[g, h][:, cols, :].rearrange("p (c i) t -> p c t i", i=4),
                     in_=d_rows[g, h][:, :, cols].rearrange("p t (c i) -> p c t i", i=4),
                 )
-            for c in range(W // CHUNK):
-                cols = slice(CHUNK * c, CHUNK * (c + 1))
-                nc.vector.quantize_mx(
-                    out=d_codes[g, h][:, cols].bitcast(FP8X4),
-                    scales=d_plane[g, h][:, cols],
-                    in_=grouped[:, cols, :].rearrange("p n t -> p (n t)"),
-                )
+
+        def quantize_d(g, h):
+            nc.vector.quantize_mx(
+                out=d_codes[g, h][:].bitcast(FP8X4),
+                scales=d_plane[g, h][:],
+                in_=d_grouped[g, h][:].rearrange("p n t -> p (n t)"),
+            )
 
         def mx_pass(bank, tile, g, rhs, rhs_scale, start, stop):
             r = tile % ROWS
@@ -158,16 +162,13 @@ def tile_two_horizon_variance_contributions_k3_kernel(
             return psum.tile([P, W], F32, name="bank")
 
         horizon1_bank = {}
-        impact_sq = {}
-        horizon1_sq = {}
-        y_sorted = {}
 
         def impact_pass(bank, tile, g, first, count):
             h = tile // ROWS
             mx_pass(
                 bank[:, 0:count], tile, g,
                 a_codes[g, h][:, first : first + count].bitcast(FP8X4),
-                a_plane[A_ROW:, g, W * h + first : W * h + first + count],
+                a_plane[h][A_ROW:, g, first : first + count],
                 g == 0, g == GROUPS - 1,
             )
 
@@ -175,7 +176,7 @@ def tile_two_horizon_variance_contributions_k3_kernel(
             h = tile // ROWS
             mx_pass(
                 horizon1_bank[tile][:], tile, g,
-                b_codes[h][:, g, :].bitcast(FP4X4), b_plane[:, g, W * h : W * (h + 1)],
+                b_codes[h][:, g, :].bitcast(FP4X4), b_plane[h][:, g, :],
                 g == 0, False,
             )
 
@@ -187,13 +188,22 @@ def tile_two_horizon_variance_contributions_k3_kernel(
                 False, g == GROUPS - 1,
             )
 
+        def pair_tiles(name, shape, dtype):
+            return [kept("%s_%d" % (name, i), [P, 2] + shape, dtype) for i in range(TILES // 2)]
+
+        impact_sq = pair_tiles("impact_sq", [W], F32)
+        horizon1_sq = pair_tiles("horizon1_sq", [W], F32)
+        y = pair_tiles("y", [W], F32)
+        y_sorted = pair_tiles("y_sorted", [W], BF16)
+
+        def part_of(pairs, tile, count=1):
+            return pairs[tile // 2][:, tile % 2 : tile % 2 + count, :]
+
         def square_impact(tile, bank):
-            impact_sq[tile] = kept("impact_sq_%d" % tile, [P, W], F32)
-            nc.scalar.activation(out=impact_sq[tile][:], in_=bank[:], func=SQUARE)
+            nc.scalar.activation(out=part_of(impact_sq, tile)[:, 0, :], in_=bank[:], func=SQUARE)
 
         def square_horizon1(tile):
-            horizon1_sq[tile] = kept("horizon1_sq_%d" % tile, [P, W], F32)
-            nc.scalar.activation(out=horizon1_sq[tile][:], in_=horizon1_bank[tile][:], func=SQUARE)
+            nc.scalar.activation(out=part_of(horizon1_sq, tile)[:, 0, :], in_=horizon1_bank[tile][:], func=SQUARE)
 
         def impact(tile):
             bank = new_bank()
@@ -211,38 +221,33 @@ def tile_two_horizon_variance_contributions_k3_kernel(
                 update_pass(tile, g)
             square_horizon1(tile)
 
-        def by_word(ap):
-            return ap.rearrange("i (p u e) -> i u p e", u=2, e=2)
-
-        y = {}
-
-        def add_squares(tile):
+        def add_squares(tile, count=1):
             h, r = divmod(tile, ROWS)
-            y[tile] = kept("y_%d" % tile, [P, W], F32)
-            nc.vector.tensor_tensor(out=y[tile][:], in0=impact_sq[tile][:], in1=horizon1_sq[tile][:], op=ADD)
-            rows = out_0[r : MIXED * P : MIXED, :] if r < MIXED else out_0[P * r : P * (r + 1), :]
-            nc.sync.dma_start(out=rows[:, W * h : W * (h + 1)], in_=y[tile][:])
+            nc.vector.tensor_tensor(
+                out=part_of(y, tile, count), in0=part_of(impact_sq, tile, count), in1=part_of(horizon1_sq, tile, count), op=ADD
+            )
+            if r < MIXED:
+                rows = out_0[0 : MIXED * P, :].rearrange("(i r) n -> i r n", r=MIXED)[:, r : r + count, :]
+            else:
+                rows = out_0[P * r : P * (r + count), :].rearrange("(r i) n -> i r n", r=count)
+            nc.sync.dma_start(out=rows[:, :, W * h : W * (h + 1)], in_=part_of(y, tile, count))
 
-        def round_y(tile):
-            y_sorted[tile] = kept("y_sorted_%d" % tile, [P, 2, P, 2], BF16)
-            nc.vector.tensor_copy(out=y_sorted[tile][:], in_=by_word(y[tile][:]))
+        def round_y(copy, tile, count=1):
+            copy(
+                out=part_of(y_sorted, tile, count).rearrange("i r (u p e) -> i r u p e", u=2, e=2),
+                in_=part_of(y, tile, count).rearrange("i r (p u e) -> i r u p e", u=2, e=2),
+            )
 
-        def finish(tiles):
-            for tile in tiles:
-                add_squares(tile)
-            for tile in tiles:
-                round_y(tile)
-
-        def sorted_words(tile):
-            return y_sorted[tile][:].rearrange("i u p e -> i (u p e)").bitcast(F32)
+        def sorted_words(tile, count=1):
+            return part_of(y_sorted, tile, count).rearrange("i r n -> i (r n)").bitcast(F32)
 
         mixed_grouped = [kept("mixed_grouped_%d" % h, [P, P, MIXED * PACK], BF16) for h in range(HALVES)]
         turned = {}
 
-        def turn_blocks(tile):
+        def turn_blocks(tile, count=1):
             if tile % 2 == 0:
-                turned[tile // 2] = kept("turned_%d" % tile, [P, 2, 2 * P], F32)
-            nc.vector.transpose(out=turned[tile // 2][:, tile % 2, :], in_=sorted_words(tile))
+                turned[tile // 2] = work.tile([P, 2, 2 * P], F32, name="turned", align_bytes=256)
+            nc.vector.transpose(out=part_of(turned, tile, count).rearrange("p r n -> p (r n)"), in_=sorted_words(tile, count))
 
         def pair_words(tile):
             h, r = divmod(tile, ROWS)
@@ -262,18 +267,20 @@ def tile_two_horizon_variance_contributions_k3_kernel(
                 in_=mixed_grouped[h][:].rearrange("p n w -> p (n w)"),
             )
 
-        def store_mixed_planes():
-            words = out_1.rearrange("h (b c) m t -> c (h b) (m t)", b=QUADS)
+        def store_mixed_words(h):
+            words = out_1[h].rearrange("(b c) m t -> c b (m t)", b=QUADS)
+            for q in PORT_ORDER:
+                nc.sync.dma_start(
+                    out=words[:, :, PACK * P * q : PACK * P * (q + 1)].bitcast(I32),
+                    in_=mixed_y_codes[QUAD * q : QUAD * (q + 1), QUADS * h : QUADS * (h + 1), :].bitcast(I32),
+                )
+
+        def store_mixed_scales():
             scales = out_2.rearrange("h (b s) m -> s (h b) m", b=QUADS)
             for q in PORT_ORDER:
                 nc.sync.dma_start(
                     out=scales[:, :, P * q : P * (q + 1)].bitcast(I32),
                     in_=mixed_y_plane[QUAD * q : QUAD * q + 4, :, :].bitcast(I32),
-                )
-            for q in PORT_ORDER:
-                nc.sync.dma_start(
-                    out=words[:, :, PACK * P * q : PACK * P * (q + 1)].bitcast(I32),
-                    in_=mixed_y_codes[QUAD * q : QUAD * (q + 1), :, :].bitcast(I32),
                 )
 
         plain = (ROWS - MIXED) * P
@@ -307,89 +314,98 @@ def tile_two_horizon_variance_contributions_k3_kernel(
         for g in range(GROUPS):
             for tile in sweep:
                 frozen_pass(tile, g)
-        prepare_d(0, 0)
+        on_vector, on_scalar = nc.vector.tensor_copy, nc.scalar.copy
         square_impact(0, impact_banks[0])
+        square_impact(1, impact_banks[1])
+        interleave_d(0, 0)
+        quantize_d(0, 0)
         for tile in sweep:
             update_pass(tile, 0)
-        prepare_d(1, 0)
-        square_impact(1, impact_banks[1])
+        interleave_d(1, 0)
+        quantize_d(1, 0)
         for tile in sweep:
             update_pass(tile, 1)
-        prepare_d(2, 0)
+        interleave_d(2, 0)
+        quantize_d(2, 0)
         square_impact(2, impact_banks[2])
         square_impact(3, impact_banks[3])
+        interleave_d(0, 1)
+        quantize_d(0, 1)
         impact(4)
+        interleave_d(1, 1)
+        quantize_d(1, 1)
         for tile in sweep:
             update_pass(tile, 2)
             square_horizon1(tile)
-
-        prepare_d(0, 1)
-        prepare_d(1, 1)
         frozen(4)
         update(4)
-        impact(6)
-        frozen(6)
-        add_squares(0)
-        add_squares(1)
-        add_squares(2)
-        prepare_d(2, 1)
-        impact(7)
-        frozen(7)
-        add_squares(3)
-        add_squares(4)
-        update(6)
-        update(7)
-        impact(8)
-        for tile in sweep:
-            round_y(tile)
-        for tile in sweep:
-            turn_blocks(tile)
-        pair_words(0)
-        pair_words(2)
-        frozen(8)
-        update(8)
-        impact(9)
-        finish([6, 7])
-        quantize_mixed(0)
-        add_squares(8)
-        turn_blocks(6)
-        turn_blocks(7)
-        round_y(8)
-        frozen(9)
-        update(9)
-        pair_words(6)
+        add_squares(0, 2)
         impact(5)
+        impact(6)
+        impact(7)
+        add_squares(2, 2)
+        round_y(on_vector, 0, 2)
+        interleave_d(2, 1)
+        round_y(on_vector, 2, 2)
+        quantize_d(2, 1)
+        impact(8)
+        impact(9)
+        turn_blocks(0, 2)
+        turn_blocks(2, 2)
+        add_squares(4)
+        frozen(6)
+        frozen(7)
+        frozen(8)
+        pair_words(0)
+        update(6)
+        pair_words(2)
+        add_squares(6)
+        quantize_mixed(0)
+        store_mixed_words(0)
+        round_y(on_vector, 6)
+        frozen(9)
+        update(7)
+        add_squares(7)
+        turn_blocks(6)
+        round_y(on_vector, 7)
+        update(8)
+        add_squares(8)
+        turn_blocks(7)
+        round_y(on_vector, 8)
+        update(9)
+        round_y(on_scalar, 4)
         add_squares(9)
         turn_blocks(8)
-        round_y(9)
-        round_y(4)
+        round_y(on_vector, 9)
+        pair_words(6)
         turn_blocks(9)
-        pair_words(8)
         frozen(5)
         update(5)
+        pair_words(8)
+        add_squares(5)
         quantize_mixed(1)
-        store_mixed_planes()
+        store_mixed_scales()
+        store_mixed_words(1)
         impact(10)
-        finish([5])
+        round_y(on_vector, 5)
         frozen(10)
         update(10)
-        finish([10])
+        add_squares(10)
+        round_y(on_vector, 10)
 
         frozen(LAST)
         update(LAST)
-        y_sorted[LAST] = kept("y_sorted_%d" % LAST, [P, 2, P, 2], BF16)
-        impact_sq[LAST] = kept("impact_sq_last", [P, W], F32)
         part = W // 2
+        last_sorted = part_of(y_sorted, LAST)[:, 0, :].rearrange("i (u p e) -> i u p e", u=2, e=2)
         for c in range(2):
             bank = new_bank()
             for g in range(GROUPS):
                 impact_pass(bank, LAST, g, part * c, part)
             cols = slice(part * c, part * (c + 1))
-            nc.scalar.activation(out=impact_sq[LAST][:, cols], in_=bank[:, 0:part], func=SQUARE)
-            nc.vector.tensor_tensor(
-                out=y_sorted[LAST][:, :, P // 2 * c : P // 2 * (c + 1), :],
-                in0=by_word(impact_sq[LAST][:, cols]), in1=by_word(horizon1_sq[LAST][:, cols]), op=ADD,
-            )
+            squares = [part_of(pairs, LAST)[:, 0, cols] for pairs in (impact_sq, horizon1_sq)]
+            nc.scalar.activation(out=squares[0], in_=bank[:, 0:part], func=SQUARE)
+            in0, in1 = [sq.rearrange("i (p u e) -> i u p e", u=2, e=2) for sq in squares]
+            nc.vector.tensor_tensor(out=last_sorted[:, :, P // 2 * c : P // 2 * (c + 1), :], in0=in0, in1=in1, op=ADD)
         add_squares(LAST)
         turn_whole((4, 5))
         turn_whole((10,))

from contextlib import ExitStack

import concourse.mybir as mybir
from concourse.masks import make_identity

M, K, N = 768, 1536, 1024
FLOPS = 3 * 2 * M * K * N

F32 = mybir.dt.float32
BF16 = mybir.dt.bfloat16
I32 = mybir.dt.int32
U32 = mybir.dt.uint32
U8 = mybir.dt.uint8
FP8X4 = mybir.dt.float8_e4m3fn_x4
FP4X4 = mybir.dt.float4_e2m1fn_x4
SQUARE = mybir.ActivationFunctionType.Square
ADD = mybir.AluOpType.add

P = 128
QUAD = 32
QUADS = P // QUAD
PACK = 4
GROUPS = K // (P * PACK)
W = 512
HALVES = N // W
ROWS = M // P
TILES = HALVES * ROWS
LAST = TILES - 1
MIXED = 4
CHUNK = 256
VECTOR_SHARE = 320
A_ROW = 4
PORT_ORDER = (0, 2, 1, 3)


def tile_two_horizon_variance_contributions_k3_kernel(
    tc, x_words, x_scales, a_words, a_scales, b_words, b_scales, d, out_0, out_1, out_2
):
    nc = tc.nc
    with ExitStack() as ctx:
        keep = ctx.enter_context(tc.tile_pool(name="keep", bufs=1))
        work = ctx.enter_context(tc.tile_pool(name="work", bufs=3))
        psum = ctx.enter_context(tc.psum_pool(name="psum", bufs=8))
        ctx.enter_context(tc.manual_schedule())

        def kept(name, shape, dtype):
            return keep.tile(shape, dtype, name=name, align_bytes=256)

        x_plane = kept("x_plane", [P, GROUPS, M], U8)
        a_plane = [kept("a_plane_%d" % h, [P, GROUPS, W], U8) for h in range(HALVES)]
        b_plane = [kept("b_plane_%d" % h, [P, GROUPS, W], U8) for h in range(HALVES)]
        for plane in (x_plane, a_plane[0], b_plane[0], a_plane[1], b_plane[1]):
            nc.vector.memset(plane[:].bitcast(I32), 0)

        def load_scale_rows(queue, plane, row, scales, quads):
            for q in quads:
                queue.dma_start(
                    out=plane[QUAD * q + row : QUAD * q + row + 4, :, :].bitcast(I32),
                    in_=scales[:, 4 * q : 4 * q + 4, :].rearrange("g r n -> r g n").bitcast(I32),
                )

        def load_words(name, words, groups, first, count):
            codes = kept(name, [P, len(groups), count], U32)
            rows = words[groups.start : groups.stop].rearrange("g p n t -> p g (n t)")
            nc.sync.dma_start(out=codes[:].bitcast(I32), in_=rows[:, :, PACK * first : PACK * (first + count)].bitcast(I32))
            return codes

        a_codes = {}
        b_codes = {}
        d_rows = {}

        def load_a(groups, h):
            codes = load_words("a_codes_%d_%d" % (groups.start, h), a_words, groups, W * h, W)
            for i, g in enumerate(groups):
                a_codes[g, h] = codes[:, i, :]

        def load_b(h):
            b_codes[h] = kept("b_codes_%d" % h, [P, GROUPS, 2 * W], U8)
            nc.sync.dma_start(
                out=b_codes[h][:].bitcast(I32),
                in_=b_words[:, :, 2 * W * h : 2 * W * (h + 1)].rearrange("g p n -> p g n").bitcast(I32),
            )

        def load_d(g, h):
            d_rows[g, h] = kept("d_rows_%d_%d" % (g, h), [P, PACK, W], BF16)
            nc.sync.dma_start(
                out=d_rows[g, h][:],
                in_=d[P * PACK * g : P * PACK * (g + 1), W * h : W * (h + 1)].rearrange("(p t) n -> p t n", t=PACK),
            )

        load_scale_rows(nc.sync, x_plane, 0, x_scales, (0,))
        load_scale_rows(nc.scalar, x_plane, 0, x_scales, (2,))
        load_scale_rows(nc.sync, x_plane, 0, x_scales, (1,))
        load_scale_rows(nc.scalar, x_plane, 0, x_scales, (3,))
        x_early = load_words("x_early", x_words, range(0, 1), 0, MIXED * P)
        load_a(range(0, 1), 0)
        load_scale_rows(nc.sync, a_plane[0], A_ROW, a_scales[:, :, 0:W], PORT_ORDER)
        x_late = load_words("x_late", x_words, range(1, 3), 0, MIXED * P)
        load_a(range(1, 2), 0)
        load_a(range(2, 3), 0)
        load_b(0)
        load_scale_rows(nc.sync, b_plane[0], 0, b_scales[:, :, 0:W], PORT_ORDER)
        for g in range(GROUPS):
            load_d(g, 0)
        x_rest = load_words("x_rest", x_words, range(GROUPS), MIXED * P, (ROWS - MIXED) * P)
        load_d(0, 1)
        load_d(1, 1)
        load_scale_rows(nc.sync, a_plane[1], A_ROW, a_scales[:, :, W:], PORT_ORDER)
        load_a(range(GROUPS), 1)
        load_scale_rows(nc.sync, b_plane[1], 0, b_scales[:, :, W:], PORT_ORDER)
        load_b(1)
        load_d(2, 1)
        identity = kept("identity", [P, P], F32)
        make_identity(nc, identity[:])
        table_warm = kept("table_warm", [P, 1], F32)
        nc.scalar.activation(out=table_warm[:], in_=identity[:, 0:1], func=SQUARE)

        mixed_codes = [kept("mixed_codes_%d" % g, [P, MIXED * P], U32) for g in range(GROUPS)]
        mixed_plane = [kept("mixed_plane_%d" % g, [P, MIXED * P], U8) for g in range(GROUPS)]
        for g, loaded in enumerate((x_early[:, 0, :], x_late[:, 0, :], x_late[:, 1, :])):
            nc.vector.tensor_copy(
                out=mixed_plane[g][:].rearrange("p (r i) -> p r i", r=MIXED),
                in_=x_plane[:, g, 0 : MIXED * P].rearrange("p (i r) -> p r i", r=MIXED),
            )
            nc.vector.tensor_copy(
                out=mixed_codes[g][:].bitcast(I32).rearrange("p (r i) -> p r i", r=MIXED),
                in_=loaded.bitcast(I32).rearrange("p (i r) -> p r i", r=MIXED),
            )

        d_codes = {(g, h): kept("d_codes_%d_%d" % (g, h), [P, W], U32) for g in range(GROUPS) for h in range(HALVES)}
        d_plane = {(g, h): kept("d_plane_%d_%d" % (g, h), [P, W], U8) for g in range(GROUPS) for h in range(HALVES)}

        d_grouped = {}

        def interleave_d(g, h):
            d_grouped[g, h] = work.tile([P, W, PACK], BF16, name="d_grouped", align_bytes=256)
            for copy, cols in ((nc.vector.tensor_copy, slice(0, VECTOR_SHARE)), (nc.scalar.copy, slice(VECTOR_SHARE, W))):
                copy(
                    out=d_grouped[g, h][:, cols, :].rearrange("p (c i) t -> p c t i", i=4),
                    in_=d_rows[g, h][:, :, cols].rearrange("p t (c i) -> p c t i", i=4),
                )

        def quantize_d(g, h):
            nc.vector.quantize_mx(
                out=d_codes[g, h][:].bitcast(FP8X4),
                scales=d_plane[g, h][:],
                in_=d_grouped[g, h][:].rearrange("p n t -> p (n t)"),
            )

        def mx_pass(bank, tile, g, rhs, rhs_scale, start, stop):
            r = tile % ROWS
            cols = slice(P * r, P * (r + 1))
            if r < MIXED:
                codes, plane = mixed_codes[g][:, cols], mixed_plane[g][:, cols]
            else:
                codes, plane = x_rest[:, g, P * (r - MIXED) : P * (r - MIXED + 1)], x_plane[:, g, cols]
            nc.tensor.matmul_mx(
                out=bank, lhsT=codes.bitcast(FP8X4), lhsT_scale=plane, rhs=rhs, rhs_scale=rhs_scale, start=start, stop=stop
            )

        def new_bank():
            return psum.tile([P, W], F32, name="bank")

        horizon1_bank = {}

        def impact_pass(bank, tile, g, first, count):
            h = tile // ROWS
            mx_pass(
                bank[:, 0:count], tile, g,
                a_codes[g, h][:, first : first + count].bitcast(FP8X4),
                a_plane[h][A_ROW:, g, first : first + count],
                g == 0, g == GROUPS - 1,
            )

        def frozen_pass(tile, g):
            h = tile // ROWS
            mx_pass(
                horizon1_bank[tile][:], tile, g,
                b_codes[h][:, g, :].bitcast(FP4X4), b_plane[h][:, g, :],
                g == 0, False,
            )

        def update_pass(tile, g):
            h = tile // ROWS
            mx_pass(
                horizon1_bank[tile][:], tile, g,
                d_codes[g, h][:].bitcast(FP8X4), d_plane[g, h][:],
                False, g == GROUPS - 1,
            )

        def pair_tiles(name, shape, dtype):
            return [kept("%s_%d" % (name, i), [P, 2] + shape, dtype) for i in range(TILES // 2)]

        impact_sq = pair_tiles("impact_sq", [W], F32)
        horizon1_sq = pair_tiles("horizon1_sq", [W], F32)
        y = pair_tiles("y", [W], F32)
        y_sorted = pair_tiles("y_sorted", [W], BF16)

        def part_of(pairs, tile, count=1):
            return pairs[tile // 2][:, tile % 2 : tile % 2 + count, :]

        def square_impact(tile, bank):
            nc.scalar.activation(out=part_of(impact_sq, tile)[:, 0, :], in_=bank[:], func=SQUARE)

        def square_horizon1(tile):
            nc.scalar.activation(out=part_of(horizon1_sq, tile)[:, 0, :], in_=horizon1_bank[tile][:], func=SQUARE)

        def impact(tile):
            bank = new_bank()
            for g in range(GROUPS):
                impact_pass(bank, tile, g, 0, W)
            square_impact(tile, bank)

        def frozen(tile):
            horizon1_bank[tile] = new_bank()
            for g in range(GROUPS):
                frozen_pass(tile, g)

        def update(tile):
            for g in range(GROUPS):
                update_pass(tile, g)
            square_horizon1(tile)

        def add_squares(tile, count=1):
            h, r = divmod(tile, ROWS)
            nc.vector.tensor_tensor(
                out=part_of(y, tile, count), in0=part_of(impact_sq, tile, count), in1=part_of(horizon1_sq, tile, count), op=ADD
            )
            if r < MIXED:
                rows = out_0[0 : MIXED * P, :].rearrange("(i r) n -> i r n", r=MIXED)[:, r : r + count, :]
            else:
                rows = out_0[P * r : P * (r + count), :].rearrange("(r i) n -> i r n", r=count)
            nc.sync.dma_start(out=rows[:, :, W * h : W * (h + 1)], in_=part_of(y, tile, count))

        def round_y(copy, tile, count=1):
            copy(
                out=part_of(y_sorted, tile, count).rearrange("i r (u p e) -> i r u p e", u=2, e=2),
                in_=part_of(y, tile, count).rearrange("i r (p u e) -> i r u p e", u=2, e=2),
            )

        def sorted_words(tile, count=1):
            return part_of(y_sorted, tile, count).rearrange("i r n -> i (r n)").bitcast(F32)

        mixed_grouped = [kept("mixed_grouped_%d" % h, [P, P, MIXED * PACK], BF16) for h in range(HALVES)]
        turned = {}

        def turn_blocks(tile, count=1):
            if tile % 2 == 0:
                turned[tile // 2] = work.tile([P, 2, 2 * P], F32, name="turned", align_bytes=256)
            nc.vector.transpose(out=part_of(turned, tile, count).rearrange("p r n -> p (r n)"), in_=sorted_words(tile, count))

        def pair_words(tile):
            h, r = divmod(tile, ROWS)
            nc.scalar.copy(
                out=mixed_grouped[h][:].bitcast(F32)[:, :, 2 * r : 2 * r + 4],
                in_=turned[tile // 2][:].rearrange("p r (u n) -> p n (r u)", u=2),
            )

        mixed_y_codes = kept("mixed_y_codes", [P, HALVES * QUADS, P], U32)
        mixed_y_plane = kept("mixed_y_plane", [P, HALVES * QUADS, P], U8)

        def quantize_mixed(h):
            blocks = slice(QUADS * h, QUADS * (h + 1))
            nc.vector.quantize_mx(
                out=mixed_y_codes[:, blocks, :].rearrange("p b i -> p (b i)").bitcast(FP8X4),
                scales=mixed_y_plane[:, blocks, :].rearrange("p b i -> p (b i)"),
                in_=mixed_grouped[h][:].rearrange("p n w -> p (n w)"),
            )

        def store_mixed_words(h):
            words = out_1[h].rearrange("(b c) m t -> c b (m t)", b=QUADS)
            for q in PORT_ORDER:
                nc.sync.dma_start(
                    out=words[:, :, PACK * P * q : PACK * P * (q + 1)].bitcast(I32),
                    in_=mixed_y_codes[QUAD * q : QUAD * (q + 1), QUADS * h : QUADS * (h + 1), :].bitcast(I32),
                )

        def store_mixed_scales():
            scales = out_2.rearrange("h (b s) m -> s (h b) m", b=QUADS)
            for q in PORT_ORDER:
                nc.sync.dma_start(
                    out=scales[:, :, P * q : P * (q + 1)].bitcast(I32),
                    in_=mixed_y_plane[QUAD * q : QUAD * q + 4, :, :].bitcast(I32),
                )

        plain = (ROWS - MIXED) * P
        plain_codes = kept("plain_y_codes", [P, HALVES, plain], U32)
        plain_plane = kept("plain_y_plane", [P, HALVES, plain], U8)

        def turn_whole(tiles):
            bank = new_bank()
            for n, tile in enumerate(tiles):
                for u in range(2):
                    nc.tensor.transpose(
                        bank[:, P * (2 * n + u) : P * (2 * n + u + 1)], sorted_words(tile)[:, P * u : P * (u + 1)], identity[:]
                    )
            h, r = divmod(tiles[0], ROWS)
            count = len(tiles)
            grouped = work.tile([P, count * P * PACK], BF16, name="plain_grouped", align_bytes=256)
            nc.scalar.copy(
                out=grouped[:].bitcast(F32).rearrange("p (n i u) -> p n i u", n=count, u=2),
                in_=bank[:, 0 : 2 * P * count].rearrange("p (n u i) -> p n i u", n=count, u=2),
            )
            cols = slice(P * (r - MIXED), P * (r - MIXED + count))
            nc.vector.quantize_mx(out=plain_codes[:, h, cols].bitcast(FP8X4), scales=plain_plane[:, h, cols], in_=grouped[:])

        sweep = range(MIXED)
        impact_banks = [new_bank() for tile in sweep]
        for g in range(GROUPS):
            for tile in sweep:
                impact_pass(impact_banks[tile], tile, g, 0, W)
        for tile in sweep:
            horizon1_bank[tile] = new_bank()
        for g in range(GROUPS):
            for tile in sweep:
                frozen_pass(tile, g)
        on_vector, on_scalar = nc.vector.tensor_copy, nc.scalar.copy
        square_impact(0, impact_banks[0])
        square_impact(1, impact_banks[1])
        interleave_d(0, 0)
        quantize_d(0, 0)
        for tile in sweep:
            update_pass(tile, 0)
        interleave_d(1, 0)
        quantize_d(1, 0)
        for tile in sweep:
            update_pass(tile, 1)
        interleave_d(2, 0)
        quantize_d(2, 0)
        square_impact(2, impact_banks[2])
        square_impact(3, impact_banks[3])
        interleave_d(0, 1)
        quantize_d(0, 1)
        impact(4)
        interleave_d(1, 1)
        quantize_d(1, 1)
        for tile in sweep:
            update_pass(tile, 2)
            square_horizon1(tile)
        frozen(4)
        update(4)
        add_squares(0, 2)
        impact(5)
        impact(6)
        impact(7)
        add_squares(2, 2)
        round_y(on_vector, 0, 2)
        interleave_d(2, 1)
        round_y(on_vector, 2, 2)
        quantize_d(2, 1)
        impact(8)
        impact(9)
        turn_blocks(0, 2)
        turn_blocks(2, 2)
        add_squares(4)
        frozen(6)
        frozen(7)
        frozen(8)
        pair_words(0)
        update(6)
        pair_words(2)
        add_squares(6)
        quantize_mixed(0)
        store_mixed_words(0)
        round_y(on_vector, 6)
        frozen(9)
        update(7)
        add_squares(7)
        turn_blocks(6)
        round_y(on_vector, 7)
        update(8)
        add_squares(8)
        turn_blocks(7)
        round_y(on_vector, 8)
        update(9)
        round_y(on_scalar, 4)
        add_squares(9)
        turn_blocks(8)
        round_y(on_vector, 9)
        pair_words(6)
        turn_blocks(9)
        frozen(5)
        update(5)
        pair_words(8)
        add_squares(5)
        quantize_mixed(1)
        store_mixed_scales()
        store_mixed_words(1)
        impact(10)
        round_y(on_vector, 5)
        frozen(10)
        update(10)
        add_squares(10)
        round_y(on_vector, 10)

        frozen(LAST)
        update(LAST)
        part = W // 2
        last_sorted = part_of(y_sorted, LAST)[:, 0, :].rearrange("i (u p e) -> i u p e", u=2, e=2)
        for c in range(2):
            bank = new_bank()
            for g in range(GROUPS):
                impact_pass(bank, LAST, g, part * c, part)
            cols = slice(part * c, part * (c + 1))
            squares = [part_of(pairs, LAST)[:, 0, cols] for pairs in (impact_sq, horizon1_sq)]
            nc.scalar.activation(out=squares[0], in_=bank[:, 0:part], func=SQUARE)
            in0, in1 = [sq.rearrange("i (p u e) -> i u p e", u=2, e=2) for sq in squares]
            nc.vector.tensor_tensor(out=last_sorted[:, :, P // 2 * c : P // 2 * (c + 1), :], in0=in0, in1=in1, op=ADD)
        add_squares(LAST)
        turn_whole((4, 5))
        turn_whole((10,))
        turn_whole((LAST,))
        nc.sync.dma_start(
            out=out_1.rearrange("h p m t -> p h (m t)")[:, :, PACK * MIXED * P :].bitcast(I32),
            in_=plain_codes[:].bitcast(I32),
        )
        for q in PORT_ORDER:
            nc.scalar.dma_start(
                out=out_2[:, 4 * q : 4 * q + 4, MIXED * P :].rearrange("h s m -> s h m").bitcast(I32),
                in_=plain_plane[QUAD * q : QUAD * q + 4, :, :].bitcast(I32),
            )
